import numpy as np
import ml_dtypes


def mxq(x, axis, fmt="e4m3"):
    dtype, down = {"e4m3": (ml_dtypes.float8_e4m3fn, 7), "e5m2": (ml_dtypes.float8_e5m2, 14)}[fmt]
    v = np.moveaxis(np.asarray(x, np.float32).astype(ml_dtypes.bfloat16).astype(np.float64), axis, -1)
    blocks = v.reshape(v.shape[:-1] + (-1, 32))
    amax = np.abs(blocks).max(-1, keepdims=True)
    byte = np.maximum(np.where(amax > 0, np.frexp(amax)[1] - 1 + 127, 0) - down, 1)
    scale = np.exp2(byte - 127.0)
    codes = (blocks / scale).astype(np.float32).astype(dtype).astype(np.float64)
    return np.moveaxis((codes * scale).reshape(v.shape), -1, axis)


WIDE = False


def mx_kscale(k):
    if not WIDE:
        return np.ones(k)
    levels = np.array([30, -30])
    if k % 512:
        return np.exp2(np.random.permutation(np.resize(levels, k // 32))).repeat(32)
    a = np.empty((k // 512, 16))
    for p in range(k // 512):
        a[p, :8] = np.random.permutation(np.resize(levels, 8))
        for g in range(8):
            far = levels[np.abs(levels - a[p, g]) >= 10]
            a[p, g + 8] = far[np.random.randint(len(far))]
    return np.exp2(a.ravel()).repeat(32)


def f64(x):
    return np.asarray(x).astype(np.float64)


E2M1 = np.array([0.0, 0.5, 1.0, 1.5, 2.0, 3.0, 4.0, 6.0, -0.0, -0.5, -1.0, -1.5, -2.0, -3.0, -4.0, -6.0])


def pack_weight(w, fmt):
    k, n = w.shape
    w = f64(np.asarray(w, np.float32).astype(ml_dtypes.bfloat16)).reshape(k // 32, 32, n)
    amax = np.abs(w).max(1)
    if fmt == "e4m3":
        byte = np.frexp(amax)[1] - 1 + 127 - 7
    else:
        mant, ex = np.frexp(amax / 6.0)
        byte = np.where(mant > 0.5, ex, ex - 1) + 127
    byte = np.clip(np.where(amax > 0, byte, 1), 1, 254)
    scaled = (w * np.exp2(127.0 - byte)[:, None, :]).reshape(k, n).astype(np.float32)
    by_word = np.ascontiguousarray(scaled.reshape(k // 512, 128, 4, n).transpose(0, 1, 3, 2))
    if fmt == "e4m3":
        words = by_word.astype(ml_dtypes.float8_e4m3fn).view(np.uint8)
    else:
        c = by_word.astype(ml_dtypes.float4_e2m1fn).view(np.uint8) & 0xF
        words = (c[..., 0::2] | (c[..., 1::2] << 4)).reshape(k // 512, 128, 2 * n)
    return np.ascontiguousarray(words), np.ascontiguousarray(byte.astype(np.uint8).reshape(k // 512, 16, n))


def unpack_weight(words, scales, fmt):
    g, _, n = scales.shape
    words = np.ascontiguousarray(words).reshape(g, 128, n, -1)
    if fmt == "e4m3":
        vals = words.view(ml_dtypes.float8_e4m3fn).astype(np.float64)
    else:
        nib = np.empty((g, 128, n, 4), np.uint8)
        nib[..., 0::2] = words & 0xF
        nib[..., 1::2] = words >> 4
        vals = E2M1[nib]
    vals = vals * np.repeat(np.exp2(scales.astype(np.float64) - 127.0), 8, axis=1)[..., None]
    return vals.transpose(0, 1, 3, 2).reshape(g * 512, n)


K, L, R, M, T = 1024, 512, 1024, 512, 1024


def setup_inputs():
    n = np.random.standard_normal
    s1 = mx_kscale(K)[:, None]
    s2 = mx_kscale(L)[:, None]
    u = mx_kscale(R)[:, None]
    p_w = pack_weight(n((R, M)) / np.sqrt(R) / u, "e2m1")
    return {
        "x": (n((K, T)) * s1).astype(np.float32),
        "wx": (n((K, R)) / np.sqrt(K) / s1 * u.T).astype(np.float32),
        "c": (n((L, T)) * s2).astype(np.float32),
        "wc": (n((L, R)) / np.sqrt(L) / s2).astype(np.float32),
        "w_words": p_w[0],
        "w_scales": p_w[1],
    }


def reference(x, wx, c, wc, w_words, w_scales):
    x_ = mxq(f64(x), 0, "e4m3")
    wx_ = mxq(f64(wx), 0, "e4m3")
    c_ = mxq(f64(c), 0, "e5m2")
    wc_ = mxq(f64(wc), 0, "e4m3")
    w_ = unpack_weight(w_words, w_scales, "e2m1")
    h_ = mxq((wx_.T @ x_) * (wc_.T @ c_), 0, "e4m3")
    y = w_.T @ h_
    return y

@@ -1,0 +1,301 @@
+from contextlib import ExitStack
+
+import concourse.mybir as mybir
+
+K, L, R, M, T = 1024, 512, 1024, 512, 1024
+FLOPS = 2 * T * (K * R + L * R + R * M)
+
+F32 = mybir.dt.float32
+BF16 = mybir.dt.bfloat16
+I32 = mybir.dt.int32
+U32 = mybir.dt.uint32
+U8 = mybir.dt.uint8
+E4M3 = mybir.dt.float8_e4m3fn_x4
+E5M2 = mybir.dt.float8_e5m2_x4
+E2M1 = mybir.dt.float4_e2m1fn_x4
+
+P = 128
+PACK = 4
+PASS = P * PACK
+HALF = 512
+CHUNK = 128
+PAIR = 256
+PX_BANKS = 5
+ACC_BANKS = 3
+
+
+def tile_mix_bilin_fm_none_kernel(tc, x, wx, c, wc, w_words, w_scales, out):
+    nc = tc.nc
+    with ExitStack() as ctx:
+        keep = ctx.enter_context(tc.tile_pool(name="keep", bufs=1))
+        stage = ctx.enter_context(tc.tile_pool(name="stage", bufs=4))
+        psum = ctx.enter_context(tc.psum_pool(name="psum", bufs=1))
+        ctx.enter_context(tc.manual_schedule())
+
+        raw = {}
+
+        def load(key, src, g, col0, width):
+            t = keep.tile([P, PACK, width], F32, name="raw_" + key)
+            rows = src[g * PASS:(g + 1) * PASS, col0:col0 + width]
+            nc.sync.dma_start(out=t[:], in_=rows.rearrange("(p k) w -> p k w", k=PACK))
+            raw[key] = t
+
+        w_plane = keep.tile([P, 2, M], U8, name="w_plane", align_bytes=64)
+        nc.gpsimd.memset(w_plane[:].bitcast(I32), 0)
+        for q in range(4):
+            nc.gpsimd.dma_start(
+                out=w_plane[32 * q:32 * q + 4].bitcast(I32),
+                in_=w_scales[:, 4 * q:4 * q + 4, :].rearrange("a r n -> r a n").bitcast(I32),
+            )
+
+        load("c0", c, 0, 0, HALF)
+        load("wc0", wc, 0, 0, PASS)
+        load("c1", c, 0, HALF, HALF)
+        load("wc1", wc, 0, PASS, PASS)
+        load("wx00", wx, 0, 0, PASS)
+        load("wx01", wx, 1, 0, PASS)
+        for q in range(2):
+            for g in range(2):
+                load("x%d%d" % (q, g), x, g, q * PAIR, PAIR)
+        for g in range(2):
+            for s in range(2):
+                load("wx1%d%d" % (g, s), wx, g, PASS + s * PAIR, PAIR)
+        for g in range(2):
+            load("x2%d" % g, x, g, 2 * PAIR, PAIR)
+        w_codes = keep.tile([P, 2, 2 * M], U8, name="w_codes", align_bytes=64)
+        nc.sync.dma_start(out=w_codes[:], in_=w_words.rearrange("a p n -> p a n"))
+        for g in range(2):
+            load("x3%d" % g, x, g, 3 * PAIR, PAIR)
+
+        grouped = {}
+        codes = {}
+        scales = {}
+
+        def copy_on(engine, dst, src):
+            if engine == "v":
+                nc.vector.tensor_copy(out=dst, in_=src)
+            else:
+                nc.scalar.copy(out=dst, in_=src)
+
+        def group_tile(key, width):
+            if key not in grouped:
+                grouped[key] = stage.tile([P, width * PACK], BF16, name="grouped", align_bytes=64)
+            return grouped[key]
+
+        def cast_act(key, engine, lo, hi):
+            width = raw[key].shape[2]
+            dst = group_tile(key, width)[:, lo * PACK:hi * PACK]
+            copy_on(
+                engine,
+                dst.rearrange("p (c i k) -> p c k i", i=4, k=PACK),
+                raw[key][:, :, lo:hi].rearrange("p k (c i) -> p c k i", i=4),
+            )
+
+        def cast_weight(key, raw_key, engine, lo, hi, m0):
+            dst = group_tile(key, PASS)[:].rearrange("p (j m k) -> p m k j", j=PACK, k=PACK)
+            copy_on(
+                engine,
+                dst[:, m0:m0 + (hi - lo) // PACK],
+                raw[raw_key][:, :, lo:hi].rearrange("p k (m j) -> p m k j", j=PACK),
+            )
+
+        def quant(key, src, fmt, lo, hi, width):
+            if key not in codes:
+                codes[key] = keep.tile([P, width], U32, name="codes_" + key, align_bytes=64)
+                scales[key] = keep.tile([P, width], U8, name="scales_" + key, align_bytes=64)
+            nc.vector.quantize_mx(
+                out=codes[key][:, lo:hi].bitcast(fmt),
+                scales=scales[key][:, lo:hi],
+                in_=src[:, lo * PACK:hi * PACK],
+            )
+
+        def quant_all(key, fmt):
+            width = grouped[key].shape[1] // PACK
+            quant(key, grouped[key], fmt, 0, width, width)
+
+        acc_count = []
+
+        def acc_bank(shape):
+            acc_count.append(0)
+            return psum.tile(shape, F32, name="acc%d" % (len(acc_count) % ACC_BANKS))
+
+        pc = {}
+
+        def pc_block(a, half):
+            pc[a, half] = keep.tile([P, PACK, HALF], F32, name="pc%d%d" % (a, half))
+            wk, ck = "wc%d" % a, "c%d" % half
+            for j in range(PACK):
+                bank = acc_bank([P, HALF])
+                nc.tensor.matmul_mx(
+                    out=bank[:],
+                    lhsT=codes[wk][:, j * P:(j + 1) * P].bitcast(E4M3),
+                    lhsT_scale=scales[wk][:, j * P:(j + 1) * P],
+                    rhs=codes[ck][:].bitcast(E5M2),
+                    rhs_scale=scales[ck][:],
+                    start=True,
+                    stop=True,
+                )
+                nc.scalar.copy(out=pc[a, half][:, j, :], in_=bank[:])
+
+        px = {}
+
+        def px_pass(a, b, g):
+            if g == 0:
+                px[a, b] = psum.tile([P, PACK, CHUNK], F32, name="px%d" % (len(px) % PX_BANKS))
+            wk, xk = "wx%d%d" % (a, g), "x%d%d" % (b // 2, g)
+            cols = slice((b % 2) * CHUNK, (b % 2 + 1) * CHUNK)
+            for j in range(PACK):
+                nc.tensor.matmul_mx(
+                    out=px[a, b][:, j, :],
+                    lhsT=codes[wk][:, j * P:(j + 1) * P].bitcast(E4M3),
+                    lhsT_scale=scales[wk][:, j * P:(j + 1) * P],
+                    rhs=codes[xk][:, cols].bitcast(E4M3),
+                    rhs_scale=scales[xk][:, cols],
+                    start=(g == 0 and j == 0),
+                    stop=(g == 1 and j == PACK - 1),
+                )
+
+        hb = {}
+
+        def mult(a, b):
+            half, t0 = b // 4, (b % 4) * CHUNK
+            if (a, half) not in hb:
+                hb[a, half] = keep.tile([P, HALF * PACK], BF16, name="hb%d%d" % (a, half), align_bytes=64)
+            dst = hb[a, half][:, t0 * PACK:(t0 + CHUNK) * PACK]
+            nc.vector.tensor_tensor(
+                out=dst.rearrange("p (c i j) -> p c j i", i=4, j=PACK),
+                in0=px[a, b][:].rearrange("p j (c i) -> p c j i", i=4),
+                in1=pc[a, half][:, :, t0:t0 + CHUNK].rearrange("p j (c i) -> p c j i", i=4),
+                op=mybir.AluOpType.mult,
+            )
+
+        def quant_h(a, b0, b1):
+            half = b0 // 4
+            quant("h%d%d" % (a, half), hb[a, half], E4M3, (b0 % 4) * CHUNK, (b0 % 4 + b1 - b0) * CHUNK, HALF)
+
+        def out_pass(dst, a, nt, half, cols, start, stop):
+            hk = "h%d%d" % (a, half)
+            nc.tensor.matmul_mx(
+                out=dst,
+                lhsT=w_codes[:, a, 2 * nt * P:2 * (nt + 1) * P].bitcast(E2M1),
+                lhsT_scale=w_plane[:, a, nt * P:(nt + 1) * P],
+                rhs=codes[hk][:, cols].bitcast(E4M3),
+                rhs_scale=scales[hk][:, cols],
+                start=start,
+                stop=stop,
+            )
+
+        def out_wide(nt):
+            bank = acc_bank([P, HALF])
+            for a in range(2):
+                out_pass(bank[:], a, nt, 0, slice(0, HALF), a == 0, a == 1)
+            res = keep.tile([P, HALF], F32, name="res_n%d" % nt)
+            nc.scalar.copy(out=res[:], in_=bank[:])
+            nc.sync.dma_start(out=out[nt * P:(nt + 1) * P, 0:HALF], in_=res[:])
+
+        def out_chunk(b):
+            bank = acc_bank([P, PACK, CHUNK])
+            cols = slice((b % 4) * CHUNK, (b % 4 + 1) * CHUNK)
+            for a in range(2):
+                for nt in range(4):
+                    out_pass(bank[:, nt, :], a, nt, 1, cols, a == 0 and nt == 0, a == 1 and nt == 3)
+            res = keep.tile([P, 4, CHUNK], F32, name="res_b%d" % b)
+            nc.scalar.copy(out=res[:], in_=bank[:])
+            nc.sync.dma_start(
+                out=out[:, b * CHUNK:(b + 1) * CHUNK].rearrange("(n p) t -> p n t", p=P), in_=res[:]
+            )
+
+        cast_act("c0", "v", 0, 320)
+        cast_act("c0", "s", 320, HALF)
+        quant_all("c0", E5M2)
+        cast_weight("wc0", "wc0", "v", 0, 320, 0)
+        cast_weight("wc0", "wc0", "s", 320, PASS, 80)
+        quant_all("wc0", E4M3)
+        pc_block(0, 0)
+        cast_act("c1", "v", 0, HALF)
+        quant_all("c1", E5M2)
+        pc_block(0, 1)
+        cast_weight("wc1", "wc1", "v", 0, PASS, 0)
+        quant_all("wc1", E4M3)
+        pc_block(1, 0)
+        pc_block(1, 1)
+        for g in range(2):
+            cast_weight("wx0%d" % g, "wx0%d" % g, "v", 0, PASS, 0)
+            quant_all("wx0%d" % g, E4M3)
+        for g in range(2):
+            cast_act("x0%d" % g, "v", 0, PAIR)
+            quant_all("x0%d" % g, E4M3)
+            px_pass(0, 0, g)
+            px_pass(0, 1, g)
+        for g in range(2):
+            cast_act("x1%d" % g, "s", 0, PAIR)
+            quant_all("x1%d" % g, E4M3)
+            px_pass(0, 2, g)
+            px_pass(0, 3, g)
+            mult(0, g)
+        cast_weight("wx10", "wx100", "s", 0, PAIR, 0)
+        cast_weight("wx10", "wx101", "v", 0, PAIR, 64)
+        mult(0, 2)
+        quant_all("wx10", E4M3)
+        mult(0, 3)
+        for b in range(4):
+            px_pass(1, b, 0)
+        cast_weight("wx11", "wx110", "s", 0, PAIR, 0)
+        cast_weight("wx11", "wx111", "v", 0, PAIR, 64)
+        for j in range(PACK):
+            quant("wx11", grouped["wx11"], E4M3, j * P, (j + 1) * P, PASS)
+        for b in range(4):
+            px_pass(1, b, 1)
+        quant_h(0, 0, 4)
+        mult(1, 0)
+        mult(1, 1)
+        cast_act("x20", "s", 0, PAIR)
+        quant_all("x20", E4M3)
+        px_pass(0, 4, 0)
+        px_pass(1, 4, 0)
+        px_pass(0, 5, 0)
+        mult(1, 2)
+        px_pass(1, 5, 0)
+        cast_act("x21", "s", 0, PAIR)
+        quant_all("x21", E4M3)
+        mult(1, 3)
+        for b in (4, 5):
+            for a in range(2):
+                px_pass(a, b, 1)
+        cast_act("x30", "s", 0, PAIR)
+        cast_act("x31", "s", 0, PAIR)
+        mult(0, 4)
+        quant_h(1, 0, 4)
+        out_wide(0)
+        out_wide(1)
+        mult(1, 4)
+        quant_all("x30", E4M3)
+        px_pass(0, 6, 0)
+        px_pass(1, 6, 0)
+        px_pass(0, 7, 0)
+        quant_h(0, 4, 5)
+        quant_h(1, 4, 5)
+        mult(0, 5)
+        quant_all("x31", E4M3)
+        out_wide(2)
+        px_pass(0, 6, 1)
+        px_pass(1, 6, 1)
+        out_wide(3)
+        px_pass(1, 7, 0)
+        px_pass(0, 7, 1)
+        px_pass(1, 7, 1)
+        mult(1, 5)
+        quant_h(0, 5, 6)
+        out_chunk(4)
+        mult(0, 6)
+        quant_h(1, 5, 6)
+        out_chunk(5)
+        mult(1, 6)
+        quant_h(0, 6, 7)
+        mult(0, 7)
+        quant_h(1, 6, 7)
+        out_chunk(6)
+        mult(1, 7)
+        quant_h(0, 7, 8)
+        quant_h(1, 7, 8)
+        out_chunk(7)

@@ -42,11 +42,6 @@ def tile_mix_bilin_fm_none_kernel(tc, x, wx, c, wc, w_words, w_scales, out):
 
         w_plane = keep.tile([P, 2, M], U8, name="w_plane", align_bytes=64)
         nc.gpsimd.memset(w_plane[:].bitcast(I32), 0)
-        for q in range(4):
-            nc.gpsimd.dma_start(
-                out=w_plane[32 * q:32 * q + 4].bitcast(I32),
-                in_=w_scales[:, 4 * q:4 * q + 4, :].rearrange("a r n -> r a n").bitcast(I32),
-            )
 
         load("c0", c, 0, 0, HALF)
         load("wc0", wc, 0, 0, PASS)
@@ -58,12 +53,16 @@ def tile_mix_bilin_fm_none_kernel(tc, x, wx, c, wc, w_words, w_scales, out):
             for g in range(2):
                 load("x%d%d" % (q, g), x, g, q * PAIR, PAIR)
         for g in range(2):
-            for s in range(2):
-                load("wx1%d%d" % (g, s), wx, g, PASS + s * PAIR, PAIR)
+            load("wx1%d" % g, wx, g, PASS, PASS)
         for g in range(2):
             load("x2%d" % g, x, g, 2 * PAIR, PAIR)
         w_codes = keep.tile([P, 2, 2 * M], U8, name="w_codes", align_bytes=64)
         nc.sync.dma_start(out=w_codes[:], in_=w_words.rearrange("a p n -> p a n"))
+        for q in range(4):
+            nc.sync.dma_start(
+                out=w_plane[32 * q:32 * q + 4].bitcast(I32),
+                in_=w_scales[:, 4 * q:4 * q + 4, :].rearrange("a r n -> r a n").bitcast(I32),
+            )
         for g in range(2):
             load("x3%d" % g, x, g, 3 * PAIR, PAIR)
 
@@ -91,13 +90,10 @@ def tile_mix_bilin_fm_none_kernel(tc, x, wx, c, wc, w_words, w_scales, out):
                 raw[key][:, :, lo:hi].rearrange("p k (c i) -> p c k i", i=4),
             )
 
-        def cast_weight(key, raw_key, engine, lo, hi, m0):
+        def cast_weight(key, engine, j0):
             dst = group_tile(key, PASS)[:].rearrange("p (j m k) -> p m k j", j=PACK, k=PACK)
-            copy_on(
-                engine,
-                dst[:, m0:m0 + (hi - lo) // PACK],
-                raw[raw_key][:, :, lo:hi].rearrange("p k (m j) -> p m k j", j=PACK),
-            )
+            src = raw[key][:].rearrange("p k (m j) -> p m k j", j=PACK)
+            copy_on(engine, dst[:, :, :, j0:j0 + 2], src[:, :, :, j0:j0 + 2])
 
         def quant(key, src, fmt, lo, hi, width):
             if key not in codes:
@@ -112,6 +108,23 @@ def tile_mix_bilin_fm_none_kernel(tc, x, wx, c, wc, w_words, w_scales, out):
         def quant_all(key, fmt):
             width = grouped[key].shape[1] // PACK
             quant(key, grouped[key], fmt, 0, width, width)
+
+        def quant_half(key, fmt, s):
+            width = grouped[key].shape[1] // PACK
+            quant(key, grouped[key], fmt, s * width // 2, (s + 1) * width // 2, width)
+
+        def prepare_weight(key, second_engine):
+            cast_weight(key, "v", 0)
+            cast_weight(key, second_engine, 2)
+            quant_half(key, E4M3, 0)
+            quant_half(key, E4M3, 1)
+
+        def prepare_act(key, fmt, second_engine):
+            width = raw[key].shape[2]
+            cast_act(key, "v", 0, width // 2)
+            cast_act(key, second_engine, width // 2, width)
+            quant_half(key, fmt, 0)
+            quant_half(key, fmt, 1)
 
         acc_count = []
 
@@ -139,12 +152,12 @@ def tile_mix_bilin_fm_none_kernel(tc, x, wx, c, wc, w_words, w_scales, out):
 
         px = {}
 
-        def px_pass(a, b, g):
+        def px_pass(a, b, g, js=range(PACK)):
             if g == 0:
                 px[a, b] = psum.tile([P, PACK, CHUNK], F32, name="px%d" % (len(px) % PX_BANKS))
             wk, xk = "wx%d%d" % (a, g), "x%d%d" % (b // 2, g)
             cols = slice((b % 2) * CHUNK, (b % 2 + 1) * CHUNK)
-            for j in range(PACK):
+            for j in js:
                 nc.tensor.matmul_mx(
                     out=px[a, b][:, j, :],
                     lhsT=codes[wk][:, j * P:(j + 1) * P].bitcast(E4M3),
@@ -163,9 +176,9 @@ def tile_mix_bilin_fm_none_kernel(tc, x, wx, c, wc, w_words, w_scales, out):
                 hb[a, half] = keep.tile([P, HALF * PACK], BF16, name="hb%d%d" % (a, half), align_bytes=64)
             dst = hb[a, half][:, t0 * PACK:(t0 + CHUNK) * PACK]
             nc.vector.tensor_tensor(
-                out=dst.rearrange("p (c i j) -> p c j i", i=4, j=PACK),
-                in0=px[a, b][:].rearrange("p j (c i) -> p c j i", i=4),
-                in1=pc[a, half][:, :, t0:t0 + CHUNK].rearrange("p j (c i) -> p c j i", i=4),
+                out=dst.rearrange("p (c i j) -> p c j i", i=2, j=PACK),
+                in0=px[a, b][:].rearrange("p j (c i) -> p c j i", i=2),
+                in1=pc[a, half][:, :, t0:t0 + CHUNK].rearrange("p j (c i) -> p c j i", i=2),
                 op=mybir.AluOpType.mult,
             )
 
@@ -205,26 +218,18 @@ def tile_mix_bilin_fm_none_kernel(tc, x, wx, c, wc, w_words, w_scales, out):
                 out=out[:, b * CHUNK:(b + 1) * CHUNK].rearrange("(n p) t -> p n t", p=P), in_=res[:]
             )
 
-        cast_act("c0", "v", 0, 320)
-        cast_act("c0", "s", 320, HALF)
-        quant_all("c0", E5M2)
-        cast_weight("wc0", "wc0", "v", 0, 320, 0)
-        cast_weight("wc0", "wc0", "s", 320, PASS, 80)
-        quant_all("wc0", E4M3)
+        prepare_act("c0", E5M2, "s")
+        prepare_weight("wc0", "s")
         pc_block(0, 0)
-        cast_act("c1", "v", 0, HALF)
-        quant_all("c1", E5M2)
+        prepare_act("c1", E5M2, "v")
         pc_block(0, 1)
-        cast_weight("wc1", "wc1", "v", 0, PASS, 0)
-        quant_all("wc1", E4M3)
+        prepare_weight("wc1", "v")
         pc_block(1, 0)
         pc_block(1, 1)
         for g in range(2):
-            cast_weight("wx0%d" % g, "wx0%d" % g, "v", 0, PASS, 0)
-            quant_all("wx0%d" % g, E4M3)
+            prepare_weight("wx0%d" % g, "v")
         for g in range(2):
-            cast_act("x0%d" % g, "v", 0, PAIR)
-            quant_all("x0%d" % g, E4M3)
+            prepare_act("x0%d" % g, E4M3, "v")
             px_pass(0, 0, g)
             px_pass(0, 1, g)
         for g in range(2):
@@ -233,20 +238,20 @@ def tile_mix_bilin_fm_none_kernel(tc, x, wx, c, wc, w_words, w_scales, out):
             px_pass(0, 2, g)
             px_pass(0, 3, g)
             mult(0, g)
-        cast_weight("wx10", "wx100", "s", 0, PAIR, 0)
-        cast_weight("wx10", "wx101", "v", 0, PAIR, 64)
+        cast_weight("wx10", "v", 0)
+        cast_weight("wx10", "s", 2)
         mult(0, 2)
         quant_all("wx10", E4M3)
         mult(0, 3)
         for b in range(4):
             px_pass(1, b, 0)
-        cast_weight("wx11", "wx110", "s", 0, PAIR, 0)
-        cast_weight("wx11", "wx111", "v", 0, PAIR, 64)
-        for j in range(PACK):
-            quant("wx11", grouped["wx11"], E4M3, j * P, (j + 1) * P, PASS)
-        for b in range(4):
-            px_pass(1, b, 1)
+        cast_weight("wx11", "v", 0)
+        cast_weight("wx11", "s", 2)
         quant_h(0, 0, 4)
+        for s in range(2):
+            quant_half("wx11", E4M3, s)
+            for b in range(4):
+                px_pass(1, b, 1, range(2 * s, 2 * s + 2))
         mult(1, 0)
         mult(1, 1)
         cast_act("x20", "s", 0, PAIR)

@@ -20,8 +20,7 @@ PASS = P * PACK
 HALF = 512
 CHUNK = 128
 PAIR = 256
-PX_BANKS = 5
-ACC_BANKS = 3
+BANKS = 8
 
 
 def tile_mix_bilin_fm_none_kernel(tc, x, wx, c, wc, w_words, w_scales, out):
@@ -34,37 +33,25 @@ def tile_mix_bilin_fm_none_kernel(tc, x, wx, c, wc, w_words, w_scales, out):
 
         raw = {}
 
-        def load(key, src, g, col0, width):
-            t = keep.tile([P, PACK, width], F32, name="raw_" + key)
+        def load(keys, src, g, col0, width):
+            t = keep.tile([P, PACK, width], F32, name="raw_" + keys[0])
             rows = src[g * PASS:(g + 1) * PASS, col0:col0 + width]
             nc.sync.dma_start(out=t[:], in_=rows.rearrange("(p k) w -> p k w", k=PACK))
-            raw[key] = t
+            share = width // len(keys)
+            for n, key in enumerate(keys):
+                raw[key] = t[:, :, n * share:(n + 1) * share]
 
         w_plane = keep.tile([P, 2, M], U8, name="w_plane", align_bytes=64)
+        w_codes = keep.tile([P, 2, 2 * M], U8, name="w_codes", align_bytes=64)
         nc.gpsimd.memset(w_plane[:].bitcast(I32), 0)
 
-        load("c0", c, 0, 0, HALF)
-        load("wc0", wc, 0, 0, PASS)
-        load("c1", c, 0, HALF, HALF)
-        load("wc1", wc, 0, PASS, PASS)
-        load("wx00", wx, 0, 0, PASS)
-        load("wx01", wx, 1, 0, PASS)
-        for q in range(2):
-            for g in range(2):
-                load("x%d%d" % (q, g), x, g, q * PAIR, PAIR)
-        for g in range(2):
-            load("wx1%d" % g, wx, g, PASS, PASS)
-        for g in range(2):
-            load("x2%d" % g, x, g, 2 * PAIR, PAIR)
-        w_codes = keep.tile([P, 2, 2 * M], U8, name="w_codes", align_bytes=64)
-        nc.sync.dma_start(out=w_codes[:], in_=w_words.rearrange("a p n -> p a n"))
-        for q in range(4):
-            nc.sync.dma_start(
-                out=w_plane[32 * q:32 * q + 4].bitcast(I32),
-                in_=w_scales[:, 4 * q:4 * q + 4, :].rearrange("a r n -> r a n").bitcast(I32),
-            )
-        for g in range(2):
-            load("x3%d" % g, x, g, 3 * PAIR, PAIR)
+        def load_w():
+            nc.sync.dma_start(out=w_codes[:], in_=w_words.rearrange("a p n -> p a n"))
+            for q in range(4):
+                nc.sync.dma_start(
+                    out=w_plane[32 * q:32 * q + 4].bitcast(I32),
+                    in_=w_scales[:, 4 * q:4 * q + 4, :].rearrange("a r n -> r a n").bitcast(I32),
+                )
 
         grouped = {}
         codes = {}
@@ -76,14 +63,13 @@ def tile_mix_bilin_fm_none_kernel(tc, x, wx, c, wc, w_words, w_scales, out):
             else:
                 nc.scalar.copy(out=dst, in_=src)
 
-        def group_tile(key, width):
+        def group_tile(key):
             if key not in grouped:
-                grouped[key] = stage.tile([P, width * PACK], BF16, name="grouped", align_bytes=64)
+                grouped[key] = stage.tile([P, raw[key].shape[2] * PACK], BF16, name="grouped", align_bytes=64)
             return grouped[key]
 
         def cast_act(key, engine, lo, hi):
-            width = raw[key].shape[2]
-            dst = group_tile(key, width)[:, lo * PACK:hi * PACK]
+            dst = group_tile(key)[:, lo * PACK:hi * PACK]
             copy_on(
                 engine,
                 dst.rearrange("p (c i k) -> p c k i", i=4, k=PACK),
@@ -91,12 +77,13 @@ def tile_mix_bilin_fm_none_kernel(tc, x, wx, c, wc, w_words, w_scales, out):
             )
 
         def cast_weight(key, engine, j0):
-            dst = group_tile(key, PASS)[:].rearrange("p (j m k) -> p m k j", j=PACK, k=PACK)
-            src = raw[key][:].rearrange("p k (m j) -> p m k j", j=PACK)
+            dst = group_tile(key)[:].rearrange("p (j m k) -> p m k j", j=PACK, k=PACK)
+            src = raw[key].rearrange("p k (m j) -> p m k j", j=PACK)
             copy_on(engine, dst[:, :, :, j0:j0 + 2], src[:, :, :, j0:j0 + 2])
 
-        def quant(key, src, fmt, lo, hi, width):
+        def quant(key, src, fmt, lo, hi):
             if key not in codes:
+                width = src.shape[1] // PACK
                 codes[key] = keep.tile([P, width], U32, name="codes_" + key, align_bytes=64)
                 scales[key] = keep.tile([P, width], U8, name="scales_" + key, align_bytes=64)
             nc.vector.quantize_mx(
@@ -106,12 +93,11 @@ def tile_mix_bilin_fm_none_kernel(tc, x, wx, c, wc, w_words, w_scales, out):
             )
 
         def quant_all(key, fmt):
-            width = grouped[key].shape[1] // PACK
-            quant(key, grouped[key], fmt, 0, width, width)
+            quant(key, grouped[key], fmt, 0, grouped[key].shape[1] // PACK)
 
         def quant_half(key, fmt, s):
             width = grouped[key].shape[1] // PACK
-            quant(key, grouped[key], fmt, s * width // 2, (s + 1) * width // 2, width)
+            quant(key, grouped[key], fmt, s * width // 2, (s + 1) * width // 2)
 
         def prepare_weight(key, second_engine):
             cast_weight(key, "v", 0)
@@ -126,40 +112,58 @@ def tile_mix_bilin_fm_none_kernel(tc, x, wx, c, wc, w_words, w_scales, out):
             quant_half(key, fmt, 0)
             quant_half(key, fmt, 1)
 
-        acc_count = []
+        free_banks = list(range(BANKS))
 
-        def acc_bank(shape):
-            acc_count.append(0)
-            return psum.tile(shape, F32, name="acc%d" % (len(acc_count) % ACC_BANKS))
+        def take_bank(shape):
+            n = free_banks.pop(0)
+            return n, psum.tile(shape, F32, name="bank%d" % n)
 
         pc = {}
 
-        def pc_block(a, half):
-            pc[a, half] = keep.tile([P, PACK, HALF], F32, name="pc%d%d" % (a, half))
+        pc_bank = {}
+
+        def pc_pass(a, half, j):
             wk, ck = "wc%d" % a, "c%d" % half
+            pc_bank[a, half, j] = take_bank([P, HALF])
+            nc.tensor.matmul_mx(
+                out=pc_bank[a, half, j][1][:],
+                lhsT=codes[wk][:, j * P:(j + 1) * P].bitcast(E4M3),
+                lhsT_scale=scales[wk][:, j * P:(j + 1) * P],
+                rhs=codes[ck][:].bitcast(E5M2),
+                rhs_scale=scales[ck][:],
+                start=True,
+                stop=True,
+            )
+
+        def pc_drain(a, half, j):
+            if j == 0:
+                pc[a, half] = keep.tile([P, PACK, HALF], F32, name="pc%d%d" % (a, half))
+            n, bank = pc_bank[a, half, j]
+            nc.scalar.copy(out=pc[a, half][:, j, :], in_=bank[:])
+            free_banks.append(n)
+
+        def pc_block(a, half):
             for j in range(PACK):
-                bank = acc_bank([P, HALF])
-                nc.tensor.matmul_mx(
-                    out=bank[:],
-                    lhsT=codes[wk][:, j * P:(j + 1) * P].bitcast(E4M3),
-                    lhsT_scale=scales[wk][:, j * P:(j + 1) * P],
-                    rhs=codes[ck][:].bitcast(E5M2),
-                    rhs_scale=scales[ck][:],
-                    start=True,
-                    stop=True,
-                )
-                nc.scalar.copy(out=pc[a, half][:, j, :], in_=bank[:])
+                pc_pass(a, half, j)
+                pc_drain(a, half, j)
 
         px = {}
+        x_piece = {}
+
+        def load_x(piece, g, b0, b1):
+            load(["x%d%d" % (piece, g)], x, g, b0 * CHUNK, (b1 - b0) * CHUNK)
+            for b in range(b0, b1):
+                x_piece[b, g] = ("x%d%d" % (piece, g), (b - b0) * CHUNK)
 
         def px_pass(a, b, g, js=range(PACK)):
-            if g == 0:
-                px[a, b] = psum.tile([P, PACK, CHUNK], F32, name="px%d" % (len(px) % PX_BANKS))
-            wk, xk = "wx%d%d" % (a, g), "x%d%d" % (b // 2, g)
-            cols = slice((b % 2) * CHUNK, (b % 2 + 1) * CHUNK)
+            if (a, b) not in px:
+                px[a, b] = take_bank([P, PACK, CHUNK])
+            wk = "wx%d%d" % (a, g)
+            xk, t0 = x_piece[b, g]
+            cols = slice(t0, t0 + CHUNK)
             for j in js:
                 nc.tensor.matmul_mx(
-                    out=px[a, b][:, j, :],
+                    out=px[a, b][1][:, j, :],
                     lhsT=codes[wk][:, j * P:(j + 1) * P].bitcast(E4M3),
                     lhsT_scale=scales[wk][:, j * P:(j + 1) * P],
                     rhs=codes[xk][:, cols].bitcast(E4M3),
@@ -175,16 +179,18 @@ def tile_mix_bilin_fm_none_kernel(tc, x, wx, c, wc, w_words, w_scales, out):
             if (a, half) not in hb:
                 hb[a, half] = keep.tile([P, HALF * PACK], BF16, name="hb%d%d" % (a, half), align_bytes=64)
             dst = hb[a, half][:, t0 * PACK:(t0 + CHUNK) * PACK]
+            n, bank = px[a, b]
             nc.vector.tensor_tensor(
                 out=dst.rearrange("p (c i j) -> p c j i", i=2, j=PACK),
-                in0=px[a, b][:].rearrange("p j (c i) -> p c j i", i=2),
+                in0=bank[:].rearrange("p j (c i) -> p c j i", i=2),
                 in1=pc[a, half][:, :, t0:t0 + CHUNK].rearrange("p j (c i) -> p c j i", i=2),
                 op=mybir.AluOpType.mult,
             )
+            free_banks.append(n)
 
         def quant_h(a, b0, b1):
             half = b0 // 4
-            quant("h%d%d" % (a, half), hb[a, half], E4M3, (b0 % 4) * CHUNK, (b0 % 4 + b1 - b0) * CHUNK, HALF)
+            quant("h%d%d" % (a, half), hb[a, half], E4M3, (b0 % 4) * CHUNK, (b0 % 4 + b1 - b0) * CHUNK)
 
         def out_pass(dst, a, nt, half, cols, start, stop):
             hk = "h%d%d" % (a, half)
@@ -198,109 +204,157 @@ def tile_mix_bilin_fm_none_kernel(tc, x, wx, c, wc, w_words, w_scales, out):
                 stop=stop,
             )
 
-        def out_wide(nt):
-            bank = acc_bank([P, HALF])
-            for a in range(2):
-                out_pass(bank[:], a, nt, 0, slice(0, HALF), a == 0, a == 1)
+        acc = {}
+
+        def out_wide(nt, a):
+            if a == 0:
+                acc[nt] = take_bank([P, HALF])
+            out_pass(acc[nt][1][:], a, nt, 0, slice(0, HALF), a == 0, a == 1)
+
+        def drain_wide(nt, engine="s"):
+            n, bank = acc[nt]
             res = keep.tile([P, HALF], F32, name="res_n%d" % nt)
-            nc.scalar.copy(out=res[:], in_=bank[:])
+            copy_on(engine, res[:], bank[:])
+            free_banks.append(n)
             nc.sync.dma_start(out=out[nt * P:(nt + 1) * P, 0:HALF], in_=res[:])
 
-        def out_chunk(b):
-            bank = acc_bank([P, PACK, CHUNK])
+        def out_chunk(b, a):
+            if a == 0:
+                acc[b] = take_bank([P, PACK, CHUNK])
             cols = slice((b % 4) * CHUNK, (b % 4 + 1) * CHUNK)
-            for a in range(2):
-                for nt in range(4):
-                    out_pass(bank[:, nt, :], a, nt, 1, cols, a == 0 and nt == 0, a == 1 and nt == 3)
-            res = keep.tile([P, 4, CHUNK], F32, name="res_b%d" % b)
-            nc.scalar.copy(out=res[:], in_=bank[:])
-            nc.sync.dma_start(
-                out=out[:, b * CHUNK:(b + 1) * CHUNK].rearrange("(n p) t -> p n t", p=P), in_=res[:]
+            for nt in range(4):
+                out_pass(acc[b][1][:, nt, :], a, nt, 1, cols, a == 0 and nt == 0, a == 1 and nt == 3)
+
+        def drain_chunks(b0, b1, queue):
+            res = keep.tile([P, 4, (b1 - b0) * CHUNK], F32, name="res_b%d" % b0)
+            for b in range(b0, b1):
+                n, bank = acc[b]
+                nc.scalar.copy(out=res[:, :, (b - b0) * CHUNK:(b - b0 + 1) * CHUNK], in_=bank[:])
+                free_banks.append(n)
+            queue.dma_start(
+                out=out[:, b0 * CHUNK:b1 * CHUNK].rearrange("(n p) t -> p n t", p=P), in_=res[:]
             )
 
-        prepare_act("c0", E5M2, "s")
+        load(["c0", "c1"], c, 0, 0, T)
+        load(["wc0", "wc1"], wc, 0, 0, R)
+        load(["wx00"], wx, 0, 0, PASS)
+        load(["wx01"], wx, 1, 0, PASS)
+        load_x(0, 0, 0, 4)
+        load_x(0, 1, 0, 4)
+        load(["wx10"], wx, 0, PASS, PASS)
+        load(["wx11"], wx, 1, PASS, PASS)
+        load_w()
+        load_x(2, 0, 4, 6)
+        load_x(2, 1, 4, 6)
+        load_x(3, 0, 6, 8)
+        load_x(3, 1, 6, 8)
+
+        cast_act("c0", "v", 0, HALF)
+        cast_act("c1", "s", 0, HALF)
+        quant_all("c0", E5M2)
+        quant_all("c1", E5M2)
         prepare_weight("wc0", "s")
+        prepare_weight("wc1", "s")
         pc_block(0, 0)
-        prepare_act("c1", E5M2, "v")
-        pc_block(0, 1)
-        prepare_weight("wc1", "v")
         pc_block(1, 0)
-        pc_block(1, 1)
+        pc_block(0, 1)
         for g in range(2):
             prepare_weight("wx0%d" % g, "v")
-        for g in range(2):
-            prepare_act("x0%d" % g, E4M3, "v")
-            px_pass(0, 0, g)
-            px_pass(0, 1, g)
-        for g in range(2):
-            cast_act("x1%d" % g, "s", 0, PAIR)
-            quant_all("x1%d" % g, E4M3)
-            px_pass(0, 2, g)
-            px_pass(0, 3, g)
-            mult(0, g)
-        cast_weight("wx10", "v", 0)
-        cast_weight("wx10", "s", 2)
-        mult(0, 2)
-        quant_all("wx10", E4M3)
-        mult(0, 3)
+        for j in range(PACK):
+            pc_pass(1, 1, j)
+        prepare_act("x00", E4M3, "v")
         for b in range(4):
-            px_pass(1, b, 0)
+            px_pass(0, b, 0)
+        pc_drain(1, 1, 0)
+        pc_drain(1, 1, 1)
+        prepare_act("x01", E4M3, "s")
+        pc_drain(1, 1, 2)
+        pc_drain(1, 1, 3)
+        for b in range(4):
+            px_pass(0, b, 1)
+        cast_weight("wx10", "s", 0)
+        cast_weight("wx10", "s", 2)
+        mult(0, 0)
+        mult(0, 1)
+        mult(0, 2)
+        quant_half("wx10", E4M3, 0)
+        for b in range(4):
+            px_pass(1, b, 0, range(2))
+        mult(0, 3)
         cast_weight("wx11", "v", 0)
+        quant_half("wx10", E4M3, 1)
+        for b in range(4):
+            px_pass(1, b, 0, range(2, 4))
         cast_weight("wx11", "s", 2)
+        quant_half("wx11", E4M3, 0)
+        for b in range(2):
+            px_pass(1, b, 1, range(2))
+        quant_half("wx11", E4M3, 1)
+        for b in range(2):
+            px_pass(1, b, 1, range(2, 4))
+        for b in range(2, 4):
+            px_pass(1, b, 1)
         quant_h(0, 0, 4)
-        for s in range(2):
-            quant_half("wx11", E4M3, s)
-            for b in range(4):
-                px_pass(1, b, 1, range(2 * s, 2 * s + 2))
+        for nt in range(4):
+            out_wide(nt, 0)
+        cast_act("x20", "s", 0, PAIR)
+        cast_act("x21", "s", 0, PAIR)
         mult(1, 0)
         mult(1, 1)
-        cast_act("x20", "s", 0, PAIR)
         quant_all("x20", E4M3)
         px_pass(0, 4, 0)
         px_pass(1, 4, 0)
-        px_pass(0, 5, 0)
         mult(1, 2)
-        px_pass(1, 5, 0)
-        cast_act("x21", "s", 0, PAIR)
-        quant_all("x21", E4M3)
+        px_pass(0, 5, 0)
         mult(1, 3)
-        for b in (4, 5):
-            for a in range(2):
-                px_pass(a, b, 1)
+        quant_all("x21", E4M3)
+        px_pass(0, 4, 1)
+        px_pass(1, 4, 1)
+        quant_h(1, 0, 4)
+        px_pass(0, 5, 1)
+        px_pass(1, 5, 0)
+        px_pass(1, 5, 1)
+        for nt in range(4):
+            out_wide(nt, 1)
         cast_act("x30", "s", 0, PAIR)
         cast_act("x31", "s", 0, PAIR)
         mult(0, 4)
-        quant_h(1, 0, 4)
-        out_wide(0)
-        out_wide(1)
         mult(1, 4)
         quant_all("x30", E4M3)
         px_pass(0, 6, 0)
         px_pass(1, 6, 0)
-        px_pass(0, 7, 0)
         quant_h(0, 4, 5)
-        quant_h(1, 4, 5)
         mult(0, 5)
+        quant_h(1, 4, 5)
         quant_all("x31", E4M3)
-        out_wide(2)
         px_pass(0, 6, 1)
         px_pass(1, 6, 1)
-        out_wide(3)
-        px_pass(1, 7, 0)
+        px_pass(0, 7, 0)
+        for nt in range(4):
+            drain_wide(nt)
+        out_chunk(4, 0)
+        out_chunk(4, 1)
+        drain_chunks(4, 5, nc.sync)
         px_pass(0, 7, 1)
-        px_pass(1, 7, 1)
         mult(1, 5)
         quant_h(0, 5, 6)
-        out_chunk(4)
         mult(0, 6)
         quant_h(1, 5, 6)
-        out_chunk(5)
+        px_pass(1, 7, 0)
+        px_pass(1, 7, 1)
+        out_chunk(5, 0)
+        out_chunk(5, 1)
+        drain_chunks(5, 6, nc.sync)
         mult(1, 6)
         quant_h(0, 6, 7)
+        out_chunk(6, 0)
         mult(0, 7)
         quant_h(1, 6, 7)
-        out_chunk(6)
+        out_chunk(6, 1)
+        drain_chunks(6, 7, nc.sync)
         mult(1, 7)
         quant_h(0, 7, 8)
+        out_chunk(7, 0)
         quant_h(1, 7, 8)
-        out_chunk(7)
+        out_chunk(7, 1)
+        drain_chunks(7, 8, nc.scalar)

from contextlib import ExitStack

import concourse.mybir as mybir

K, L, R, M, T = 1024, 512, 1024, 512, 1024
FLOPS = 2 * T * (K * R + L * R + R * M)

F32 = mybir.dt.float32
BF16 = mybir.dt.bfloat16
I32 = mybir.dt.int32
U32 = mybir.dt.uint32
U8 = mybir.dt.uint8
E4M3 = mybir.dt.float8_e4m3fn_x4
E5M2 = mybir.dt.float8_e5m2_x4
E2M1 = mybir.dt.float4_e2m1fn_x4

P = 128
PACK = 4
PASS = P * PACK
HALF = 512
CHUNK = 128
PAIR = 256
BANKS = 8


def tile_mix_bilin_fm_none_kernel(tc, x, wx, c, wc, w_words, w_scales, out):
    nc = tc.nc
    with ExitStack() as ctx:
        keep = ctx.enter_context(tc.tile_pool(name="keep", bufs=1))
        stage = ctx.enter_context(tc.tile_pool(name="stage", bufs=4))
        psum = ctx.enter_context(tc.psum_pool(name="psum", bufs=1))
        ctx.enter_context(tc.manual_schedule())

        raw = {}

        def load(keys, src, g, col0, width):
            t = keep.tile([P, PACK, width], F32, name="raw_" + keys[0])
            rows = src[g * PASS:(g + 1) * PASS, col0:col0 + width]
            nc.sync.dma_start(out=t[:], in_=rows.rearrange("(p k) w -> p k w", k=PACK))
            share = width // len(keys)
            for n, key in enumerate(keys):
                raw[key] = t[:, :, n * share:(n + 1) * share]

        w_plane = keep.tile([P, 2, M], U8, name="w_plane", align_bytes=64)
        w_codes = keep.tile([P, 2, 2 * M], U8, name="w_codes", align_bytes=64)
        nc.gpsimd.memset(w_plane[:].bitcast(I32), 0)

        def load_w():
            nc.sync.dma_start(out=w_codes[:], in_=w_words.rearrange("a p n -> p a n"))
            for q in range(4):
                nc.sync.dma_start(
                    out=w_plane[32 * q:32 * q + 4].bitcast(I32),
                    in_=w_scales[:, 4 * q:4 * q + 4, :].rearrange("a r n -> r a n").bitcast(I32),
                )

        grouped = {}
        codes = {}
        scales = {}

        def copy_on(engine, dst, src):
            if engine == "v":
                nc.vector.tensor_copy(out=dst, in_=src)
            else:
                nc.scalar.copy(out=dst, in_=src)

        def group_tile(key):
            if key not in grouped:
                grouped[key] = stage.tile([P, raw[key].shape[2] * PACK], BF16, name="grouped", align_bytes=64)
            return grouped[key]

        def cast_act(key, engine, lo, hi):
            dst = group_tile(key)[:, lo * PACK:hi * PACK]
            copy_on(
                engine,
                dst.rearrange("p (c i k) -> p c k i", i=4, k=PACK),
                raw[key][:, :, lo:hi].rearrange("p k (c i) -> p c k i", i=4),
            )

        def cast_weight(key, engine, j0):
            dst = group_tile(key)[:].rearrange("p (j m k) -> p m k j", j=PACK, k=PACK)
            src = raw[key].rearrange("p k (m j) -> p m k j", j=PACK)
            copy_on(engine, dst[:, :, :, j0:j0 + 2], src[:, :, :, j0:j0 + 2])

        def quant(key, src, fmt, lo, hi):
            if key not in codes:
                width = src.shape[1] // PACK
                codes[key] = keep.tile([P, width], U32, name="codes_" + key, align_bytes=64)
                scales[key] = keep.tile([P, width], U8, name="scales_" + key, align_bytes=64)
            nc.vector.quantize_mx(
                out=codes[key][:, lo:hi].bitcast(fmt),
                scales=scales[key][:, lo:hi],
                in_=src[:, lo * PACK:hi * PACK],
            )

        def quant_all(key, fmt):
            quant(key, grouped[key], fmt, 0, grouped[key].shape[1] // PACK)

        def quant_half(key, fmt, s):
            width = grouped[key].shape[1] // PACK
            quant(key, grouped[key], fmt, s * width // 2, (s + 1) * width // 2)

        def prepare_weight(key, second_engine):
            cast_weight(key, "v", 0)
            cast_weight(key, second_engine, 2)
            quant_half(key, E4M3, 0)
            quant_half(key, E4M3, 1)

        def prepare_act(key, fmt, second_engine):
            width = raw[key].shape[2]
            cast_act(key, "v", 0, width // 2)
            cast_act(key, second_engine, width // 2, width)
            quant_half(key, fmt, 0)
            quant_half(key, fmt, 1)

        free_banks = list(range(BANKS))

        def take_bank(shape):
            n = free_banks.pop(0)
            return n, psum.tile(shape, F32, name="bank%d" % n)

        pc = {}

        pc_bank = {}

        def pc_pass(a, half, j):
            wk, ck = "wc%d" % a, "c%d" % half
            pc_bank[a, half, j] = take_bank([P, HALF])
            nc.tensor.matmul_mx(
                out=pc_bank[a, half, j][1][:],
                lhsT=codes[wk][:, j * P:(j + 1) * P].bitcast(E4M3),
                lhsT_scale=scales[wk][:, j * P:(j + 1) * P],
                rhs=codes[ck][:].bitcast(E5M2),
                rhs_scale=scales[ck][:],
                start=True,
                stop=True,
            )

        def pc_drain(a, half, j):
            if j == 0:
                pc[a, half] = keep.tile([P, PACK, HALF], F32, name="pc%d%d" % (a, half))
            n, bank = pc_bank[a, half, j]
            nc.scalar.copy(out=pc[a, half][:, j, :], in_=bank[:])
            free_banks.append(n)

        def pc_block(a, half):
            for j in range(PACK):
                pc_pass(a, half, j)
                pc_drain(a, half, j)

        px = {}
        x_piece = {}

        def load_x(piece, g, b0, b1):
            load(["x%d%d" % (piece, g)], x, g, b0 * CHUNK, (b1 - b0) * CHUNK)
            for b in range(b0, b1):
                x_piece[b, g] = ("x%d%d" % (piece, g), (b - b0) * CHUNK)

        def px_pass(a, b, g, js=range(PACK)):
            if (a, b) not in px:
                px[a, b] = take_bank([P, PACK, CHUNK])
            wk = "wx%d%d" % (a, g)
            xk, t0 = x_piece[b, g]
            cols = slice(t0, t0 + CHUNK)
            for j in js:
                nc.tensor.matmul_mx(
                    out=px[a, b][1][:, j, :],
                    lhsT=codes[wk][:, j * P:(j + 1) * P].bitcast(E4M3),
                    lhsT_scale=scales[wk][:, j * P:(j + 1) * P],
                    rhs=codes[xk][:, cols].bitcast(E4M3),
                    rhs_scale=scales[xk][:, cols],
                    start=(g == 0 and j == 0),
                    stop=(g == 1 and j == PACK - 1),
                )

        hb = {}

        def mult(a, b):
            half, t0 = b // 4, (b % 4) * CHUNK
            if (a, half) not in hb:
                hb[a, half] = keep.tile([P, HALF * PACK], BF16, name="hb%d%d" % (a, half), align_bytes=64)
            dst = hb[a, half][:, t0 * PACK:(t0 + CHUNK) * PACK]
            n, bank = px[a, b]
            nc.vector.tensor_tensor(
                out=dst.rearrange("p (c i j) -> p c j i", i=2, j=PACK),
                in0=bank[:].rearrange("p j (c i) -> p c j i", i=2),
                in1=pc[a, half][:, :, t0:t0 + CHUNK].rearrange("p j (c i) -> p c j i", i=2),
                op=mybir.AluOpType.mult,
            )
            free_banks.append(n)

        def quant_h(a, b0, b1):
            half = b0 // 4
            quant("h%d%d" % (a, half), hb[a, half], E4M3, (b0 % 4) * CHUNK, (b0 % 4 + b1 - b0) * CHUNK)

        def out_pass(dst, a, nt, half, cols, start, stop):
            hk = "h%d%d" % (a, half)
            nc.tensor.matmul_mx(
                out=dst,
                lhsT=w_codes[:, a, 2 * nt * P:2 * (nt + 1) * P].bitcast(E2M1),
                lhsT_scale=w_plane[:, a, nt * P:(nt + 1) * P],
                rhs=codes[hk][:, cols].bitcast(E4M3),
                rhs_scale=scales[hk][:, cols],
                start=start,
                stop=stop,
            )

        acc = {}

        def out_wide(nt, a):
            if a == 0:
                acc[nt] = take_bank([P, HALF])
            out_pass(acc[nt][1][:], a, nt, 0, slice(0, HALF), a == 0, a == 1)

        def drain_wide(nt, engine="s"):
            n, bank = acc[nt]
            res = keep.tile([P, HALF], F32, name="res_n%d" % nt)
            copy_on(engine, res[:], bank[:])
            free_banks.append(n)
            nc.sync.dma_start(out=out[nt * P:(nt + 1) * P, 0:HALF], in_=res[:])

        def out_chunk(b, a):
            if a == 0:
                acc[b] = take_bank([P, PACK, CHUNK])
            cols = slice((b % 4) * CHUNK, (b % 4 + 1) * CHUNK)
            for nt in range(4):
                out_pass(acc[b][1][:, nt, :], a, nt, 1, cols, a == 0 and nt == 0, a == 1 and nt == 3)

        def drain_chunks(b0, b1, queue):
            res = keep.tile([P, 4, (b1 - b0) * CHUNK], F32, name="res_b%d" % b0)
            for b in range(b0, b1):
                n, bank = acc[b]
                nc.scalar.copy(out=res[:, :, (b - b0) * CHUNK:(b - b0 + 1) * CHUNK], in_=bank[:])
                free_banks.append(n)
            queue.dma_start(
                out=out[:, b0 * CHUNK:b1 * CHUNK].rearrange("(n p) t -> p n t", p=P), in_=res[:]
            )

        load(["c0", "c1"], c, 0, 0, T)
        load(["wc0", "wc1"], wc, 0, 0, R)
        load(["wx00"], wx, 0, 0, PASS)
        load(["wx01"], wx, 1, 0, PASS)
        load_x(0, 0, 0, 4)
        load_x(0, 1, 0, 4)
        load(["wx10"], wx, 0, PASS, PASS)
        load(["wx11"], wx, 1, PASS, PASS)
        load_w()
        load_x(2, 0, 4, 6)
        load_x(2, 1, 4, 6)
        load_x(3, 0, 6, 8)
        load_x(3, 1, 6, 8)

        cast_act("c0", "v", 0, HALF)
        cast_act("c1", "s", 0, HALF)
        quant_all("c0", E5M2)
        quant_all("c1", E5M2)
        prepare_weight("wc0", "s")
        prepare_weight("wc1", "s")
        pc_block(0, 0)
        pc_block(1, 0)
        pc_block(0, 1)
        for g in range(2):
            prepare_weight("wx0%d" % g, "v")
        for j in range(PACK):
            pc_pass(1, 1, j)
        prepare_act("x00", E4M3, "v")
        for b in range(4):
            px_pass(0, b, 0)
        pc_drain(1, 1, 0)
        pc_drain(1, 1, 1)
        prepare_act("x01", E4M3, "s")
        pc_drain(1, 1, 2)
        pc_drain(1, 1, 3)
        for b in range(4):
            px_pass(0, b, 1)
        cast_weight("wx10", "s", 0)
        cast_weight("wx10", "s", 2)
        mult(0, 0)
        mult(0, 1)
        mult(0, 2)
        quant_half("wx10", E4M3, 0)
        for b in range(4):
            px_pass(1, b, 0, range(2))
        mult(0, 3)
        cast_weight("wx11", "v", 0)
        quant_half("wx10", E4M3, 1)
        for b in range(4):
            px_pass(1, b, 0, range(2, 4))
        cast_weight("wx11", "s", 2)
        quant_half("wx11", E4M3, 0)
        for b in range(2):
            px_pass(1, b, 1, range(2))
        quant_half("wx11", E4M3, 1)
        for b in range(2):
            px_pass(1, b, 1, range(2, 4))
        for b in range(2, 4):
            px_pass(1, b, 1)
        quant_h(0, 0, 4)
        for nt in range(4):
            out_wide(nt, 0)
        cast_act("x20", "s", 0, PAIR)
        cast_act("x21", "s", 0, PAIR)
        mult(1, 0)
        mult(1, 1)
        quant_all("x20", E4M3)
        px_pass(0, 4, 0)
        px_pass(1, 4, 0)
        mult(1, 2)
        px_pass(0, 5, 0)
        mult(1, 3)
        quant_all("x21", E4M3)
        px_pass(0, 4, 1)
        px_pass(1, 4, 1)
        quant_h(1, 0, 4)
        px_pass(0, 5, 1)
        px_pass(1, 5, 0)
        px_pass(1, 5, 1)
        for nt in range(4):
            out_wide(nt, 1)
        cast_act("x30", "s", 0, PAIR)
        cast_act("x31", "s", 0, PAIR)
        mult(0, 4)
        mult(1, 4)
        quant_all("x30", E4M3)
        px_pass(0, 6, 0)
        px_pass(1, 6, 0)
        quant_h(0, 4, 5)
        mult(0, 5)
        quant_h(1, 4, 5)
        quant_all("x31", E4M3)
        px_pass(0, 6, 1)
        px_pass(1, 6, 1)
        px_pass(0, 7, 0)
        for nt in range(4):
            drain_wide(nt)
        out_chunk(4, 0)
        out_chunk(4, 1)
        drain_chunks(4, 5, nc.sync)
        px_pass(0, 7, 1)
        mult(1, 5)
        quant_h(0, 5, 6)
        mult(0, 6)
        quant_h(1, 5, 6)
        px_pass(1, 7, 0)
        px_pass(1, 7, 1)
        out_chunk(5, 0)
        out_chunk(5, 1)
        drain_chunks(5, 6, nc.sync)
        mult(1, 6)
        quant_h(0, 6, 7)
        out_chunk(6, 0)
        mult(0, 7)
        quant_h(1, 6, 7)
        out_chunk(6, 1)
        drain_chunks(6, 7, nc.sync)
        mult(1, 7)
        quant_h(0, 7, 8)
        out_chunk(7, 0)
        quant_h(1, 7, 8)
        out_chunk(7, 1)
        drain_chunks(7, 8, nc.scalar)
